import numpy as np
import ml_dtypes

BF16 = ml_dtypes.bfloat16


def bf(x):
    return np.asarray(x, np.float32).astype(BF16)


def f32(x):
    return np.asarray(x, np.float32)


def f64(x):
    return np.asarray(x).astype(np.float64)


def striped(idx):
    return np.concatenate([l.reshape(-1, 16).T for l in idx])


def rows(idx, k):
    return np.tile(np.repeat(idx, 16, axis=0), (k // (16 * 8), 1))


def look(tab, idx):
    return np.take_along_axis(f64(tab), rows(idx, len(tab)), axis=1)


K, S, V, N, M = 512, 2048, 1024, 1024, 512


def setup_inputs():
    return {"tab": bf(np.random.standard_normal((2, K, S))), "x0": bf(np.random.standard_normal((K, V))), "w": bf(np.random.standard_normal((K, M)) / np.sqrt(K)), "offs": striped(np.random.randint(0, S, (8, N)))}


def reference(tab, x0, w, offs):
    idx = np.stack([g.T.reshape(-1) for g in np.split(offs, 8)])
    x = f64(x0) * look(tab[0], idx) + look(tab[1], idx)
    y = f64(w).T @ x
    return y

@@ -1,0 +1,73 @@
+import concourse.mybir as mybir
+
+P = 128
+R = 512
+S = 2048
+N = 1024
+M = 512
+HALF = 512
+BLOCKS = R // P
+HALVES = N // HALF
+OUT_BLOCKS = M // P
+OFFS_COLS = HALF // 16
+
+FLOPS = 2 * M * R * N + 2 * R * N
+
+BF16, F32, U16 = mybir.dt.bfloat16, mybir.dt.float32, mybir.dt.uint16
+MULT, ADD = mybir.AluOpType.mult, mybir.AluOpType.add
+
+
+def tile_lookup_film_mul_none_kernel(tc, tab, x0, w, offs, out):
+    nc = tc.nc
+    with (
+        tc.tile_pool(name="held", bufs=1) as held,
+        tc.psum_pool(name="psum", bufs=1) as psum,
+    ):
+        offsets = held.tile([P, N // 16], U16, name="offsets")
+        nc.sync.dma_start(offsets[:], offs)
+
+        gains, shifts, features, weights = [], [], [], []
+        for k in range(BLOCKS):
+            rows = slice(k * P, (k + 1) * P)
+            gain = held.tile([P, S], BF16, name=f"gain{k}")
+            nc.sync.dma_start(gain[:], tab[0, rows, :])
+            feature = held.tile([P, N], BF16, name=f"feature{k}")
+            nc.sync.dma_start(feature[:], x0[rows, :])
+            shift = held.tile([P, S], BF16, name=f"shift{k}")
+            nc.sync.dma_start(shift[:], tab[1, rows, :])
+            weight = held.tile([P, M], BF16, name=f"weight{k}")
+            nc.sync.dma_start(weight[:], w[rows, :])
+            gains.append(gain)
+            features.append(feature)
+            shifts.append(shift)
+            weights.append(weight)
+
+        banks = [
+            [psum.tile([P, HALF], F32, name=f"bank{h}_{m}") for m in range(OUT_BLOCKS)]
+            for h in range(HALVES)
+        ]
+        for k in range(BLOCKS):
+            for h in range(HALVES):
+                cols = slice(h * HALF, (h + 1) * HALF)
+                half_list = offsets[:, h * OFFS_COLS : (h + 1) * OFFS_COLS]
+                product = held.tile([P, HALF], BF16, name=f"product{k}_{h}")
+                nc.vector.tensor_tensor(product[:], gains[k][:].indirect(half_list), features[k][:, cols], MULT)
+                x = held.tile([P, HALF], BF16, name=f"x{k}_{h}")
+                nc.vector.tensor_tensor(x[:], shifts[k][:].indirect(half_list), product[:], ADD)
+                for m in range(OUT_BLOCKS):
+                    nc.tensor.matmul(
+                        banks[h][m][:],
+                        weights[k][:, m * P : (m + 1) * P],
+                        x[:],
+                        start=(k == 0),
+                        stop=(k == BLOCKS - 1),
+                    )
+
+        for h in range(HALVES):
+            for m in range(OUT_BLOCKS):
+                result = held.tile([P, HALF], F32, name=f"result{h}_{m}")
+                if h == HALVES - 1 and m % 2 == 0:
+                    nc.vector.tensor_copy(result[:], banks[h][m][:])
+                else:
+                    nc.scalar.copy(result[:], banks[h][m][:])
+                nc.sync.dma_start(out[m * P : (m + 1) * P, h * HALF : (h + 1) * HALF], result[:])

@@ -46,14 +46,30 @@ def tile_lookup_film_mul_none_kernel(tc, tab, x0, w, offs, out):
             [psum.tile([P, HALF], F32, name=f"bank{h}_{m}") for m in range(OUT_BLOCKS)]
             for h in range(HALVES)
         ]
-        for k in range(BLOCKS):
-            for h in range(HALVES):
-                cols = slice(h * HALF, (h + 1) * HALF)
-                half_list = offsets[:, h * OFFS_COLS : (h + 1) * OFFS_COLS]
+        early, late = range(BLOCKS // 2), range(BLOCKS // 2, BLOCKS)
+        units = [(k, h) for k in early for h in range(HALVES)] + [(k, h) for h in range(HALVES) for k in late]
+
+        products = {}
+        for step in range(len(units) + 1):
+            if step < len(units):
+                k, h = units[step]
                 product = held.tile([P, HALF], BF16, name=f"product{k}_{h}")
-                nc.vector.tensor_tensor(product[:], gains[k][:].indirect(half_list), features[k][:, cols], MULT)
+                nc.vector.tensor_tensor(
+                    product[:],
+                    gains[k][:].indirect(offsets[:, h * OFFS_COLS : (h + 1) * OFFS_COLS]),
+                    features[k][:, h * HALF : (h + 1) * HALF],
+                    MULT,
+                )
+                products[k, h] = product
+            if step > 0:
+                k, h = units[step - 1]
                 x = held.tile([P, HALF], BF16, name=f"x{k}_{h}")
-                nc.vector.tensor_tensor(x[:], shifts[k][:].indirect(half_list), product[:], ADD)
+                nc.vector.tensor_tensor(
+                    x[:],
+                    shifts[k][:].indirect(offsets[:, h * OFFS_COLS : (h + 1) * OFFS_COLS]),
+                    products[k, h][:],
+                    ADD,
+                )
                 for m in range(OUT_BLOCKS):
                     nc.tensor.matmul(
                         banks[h][m][:],

@@ -26,58 +26,55 @@ def tile_lookup_film_mul_none_kernel(tc, tab, x0, w, offs, out):
         offsets = held.tile([P, N // 16], U16, name="offsets")
         nc.sync.dma_start(offsets[:], offs)
 
-        gains, shifts, features, weights = [], [], [], []
+        gains, shifts, features = [], [], []
         for k in range(BLOCKS):
             rows = slice(k * P, (k + 1) * P)
             gain = held.tile([P, S], BF16, name=f"gain{k}")
             nc.sync.dma_start(gain[:], tab[0, rows, :])
             feature = held.tile([P, N], BF16, name=f"feature{k}")
-            nc.sync.dma_start(feature[:], x0[rows, :])
+            if k == 0:
+                for h in range(HALVES):
+                    cols = slice(h * HALF, (h + 1) * HALF)
+                    nc.scalar.dma_start(feature[:, cols], x0[rows, cols])
+            else:
+                nc.sync.dma_start(feature[:], x0[rows, :])
             shift = held.tile([P, S], BF16, name=f"shift{k}")
             nc.sync.dma_start(shift[:], tab[1, rows, :])
-            weight = held.tile([P, M], BF16, name=f"weight{k}")
-            nc.sync.dma_start(weight[:], w[rows, :])
+            if k == 0:
+                weights = held.tile([P, BLOCKS, M], BF16, name="weights")
+                nc.sync.dma_start(weights[:], w.rearrange("(k p) m -> p k m", p=P))
             gains.append(gain)
             features.append(feature)
             shifts.append(shift)
-            weights.append(weight)
 
         banks = [
             [psum.tile([P, HALF], F32, name=f"bank{h}_{m}") for m in range(OUT_BLOCKS)]
             for h in range(HALVES)
         ]
         early, late = range(BLOCKS // 2), range(BLOCKS // 2, BLOCKS)
-        units = [(k, h) for k in early for h in range(HALVES)] + [(k, h) for h in range(HALVES) for k in late]
+        units = [(k, h) for k in early for h in range(HALVES)]
+        units += [(k, 0) for k in late] + [(k, 1) for k in reversed(late)]
 
-        products = {}
-        for step in range(len(units) + 1):
-            if step < len(units):
-                k, h = units[step]
+        late_products = [held.tile([P, HALF], BF16, name=f"late_product{i}") for i in range(2)]
+        for k, h in units:
+            half_list = offsets[:, h * OFFS_COLS : (h + 1) * OFFS_COLS]
+            if k in early:
                 product = held.tile([P, HALF], BF16, name=f"product{k}_{h}")
-                nc.vector.tensor_tensor(
-                    product[:],
-                    gains[k][:].indirect(offsets[:, h * OFFS_COLS : (h + 1) * OFFS_COLS]),
-                    features[k][:, h * HALF : (h + 1) * HALF],
-                    MULT,
-                )
-                products[k, h] = product
-            if step > 0:
-                k, h = units[step - 1]
-                x = held.tile([P, HALF], BF16, name=f"x{k}_{h}")
-                nc.vector.tensor_tensor(
+            else:
+                product = late_products[(k + h) % 2]
+            nc.vector.tensor_tensor(
+                product[:], gains[k][:].indirect(half_list), features[k][:, h * HALF : (h + 1) * HALF], MULT
+            )
+            x = held.tile([P, HALF], BF16, name=f"x{k}_{h}")
+            nc.vector.tensor_tensor(x[:], shifts[k][:].indirect(half_list), product[:], ADD)
+            for m in range(OUT_BLOCKS):
+                nc.tensor.matmul(
+                    banks[h][m][:],
+                    weights[:, k, m * P : (m + 1) * P],
                     x[:],
-                    shifts[k][:].indirect(offsets[:, h * OFFS_COLS : (h + 1) * OFFS_COLS]),
-                    products[k, h][:],
-                    ADD,
+                    start=(k == early[0]),
+                    stop=(k == (late[-1] if h == 0 else late[0])),
                 )
-                for m in range(OUT_BLOCKS):
-                    nc.tensor.matmul(
-                        banks[h][m][:],
-                        weights[k][:, m * P : (m + 1) * P],
-                        x[:],
-                        start=(k == 0),
-                        stop=(k == BLOCKS - 1),
-                    )
 
         for h in range(HALVES):
             for m in range(OUT_BLOCKS):

@@ -55,17 +55,17 @@ def tile_lookup_film_mul_none_kernel(tc, tab, x0, w, offs, out):
         units = [(k, h) for k in early for h in range(HALVES)]
         units += [(k, 0) for k in late] + [(k, 1) for k in reversed(late)]
 
-        late_products = [held.tile([P, HALF], BF16, name=f"late_product{i}") for i in range(2)]
+        late_x = [held.tile([P, HALF], BF16, name=f"late_x{i}") for i in range(2)]
         for k, h in units:
             half_list = offsets[:, h * OFFS_COLS : (h + 1) * OFFS_COLS]
-            if k in early:
-                product = held.tile([P, HALF], BF16, name=f"product{k}_{h}")
-            else:
-                product = late_products[(k + h) % 2]
+            product = held.tile([P, HALF], BF16, name=f"product{k}_{h}")
             nc.vector.tensor_tensor(
                 product[:], gains[k][:].indirect(half_list), features[k][:, h * HALF : (h + 1) * HALF], MULT
             )
-            x = held.tile([P, HALF], BF16, name=f"x{k}_{h}")
+            if k in early:
+                x = held.tile([P, HALF], BF16, name=f"x{k}_{h}")
+            else:
+                x = late_x[(k + h) % 2]
             nc.vector.tensor_tensor(x[:], shifts[k][:].indirect(half_list), product[:], ADD)
             for m in range(OUT_BLOCKS):
                 nc.tensor.matmul(

import concourse.mybir as mybir

P = 128
R = 512
S = 2048
N = 1024
M = 512
HALF = 512
BLOCKS = R // P
HALVES = N // HALF
OUT_BLOCKS = M // P
OFFS_COLS = HALF // 16

FLOPS = 2 * M * R * N + 2 * R * N

BF16, F32, U16 = mybir.dt.bfloat16, mybir.dt.float32, mybir.dt.uint16
MULT, ADD = mybir.AluOpType.mult, mybir.AluOpType.add


def tile_lookup_film_mul_none_kernel(tc, tab, x0, w, offs, out):
    nc = tc.nc
    with (
        tc.tile_pool(name="held", bufs=1) as held,
        tc.psum_pool(name="psum", bufs=1) as psum,
    ):
        offsets = held.tile([P, N // 16], U16, name="offsets")
        nc.sync.dma_start(offsets[:], offs)

        gains, shifts, features = [], [], []
        for k in range(BLOCKS):
            rows = slice(k * P, (k + 1) * P)
            gain = held.tile([P, S], BF16, name=f"gain{k}")
            nc.sync.dma_start(gain[:], tab[0, rows, :])
            feature = held.tile([P, N], BF16, name=f"feature{k}")
            if k == 0:
                for h in range(HALVES):
                    cols = slice(h * HALF, (h + 1) * HALF)
                    nc.scalar.dma_start(feature[:, cols], x0[rows, cols])
            else:
                nc.sync.dma_start(feature[:], x0[rows, :])
            shift = held.tile([P, S], BF16, name=f"shift{k}")
            nc.sync.dma_start(shift[:], tab[1, rows, :])
            if k == 0:
                weights = held.tile([P, BLOCKS, M], BF16, name="weights")
                nc.sync.dma_start(weights[:], w.rearrange("(k p) m -> p k m", p=P))
            gains.append(gain)
            features.append(feature)
            shifts.append(shift)

        banks = [
            [psum.tile([P, HALF], F32, name=f"bank{h}_{m}") for m in range(OUT_BLOCKS)]
            for h in range(HALVES)
        ]
        early, late = range(BLOCKS // 2), range(BLOCKS // 2, BLOCKS)
        units = [(k, h) for k in early for h in range(HALVES)]
        units += [(k, 0) for k in late] + [(k, 1) for k in reversed(late)]

        late_x = [held.tile([P, HALF], BF16, name=f"late_x{i}") for i in range(2)]
        for k, h in units:
            half_list = offsets[:, h * OFFS_COLS : (h + 1) * OFFS_COLS]
            product = held.tile([P, HALF], BF16, name=f"product{k}_{h}")
            nc.vector.tensor_tensor(
                product[:], gains[k][:].indirect(half_list), features[k][:, h * HALF : (h + 1) * HALF], MULT
            )
            if k in early:
                x = held.tile([P, HALF], BF16, name=f"x{k}_{h}")
            else:
                x = late_x[(k + h) % 2]
            nc.vector.tensor_tensor(x[:], shifts[k][:].indirect(half_list), product[:], ADD)
            for m in range(OUT_BLOCKS):
                nc.tensor.matmul(
                    banks[h][m][:],
                    weights[:, k, m * P : (m + 1) * P],
                    x[:],
                    start=(k == early[0]),
                    stop=(k == (late[-1] if h == 0 else late[0])),
                )

        for h in range(HALVES):
            for m in range(OUT_BLOCKS):
                result = held.tile([P, HALF], F32, name=f"result{h}_{m}")
                if h == HALVES - 1 and m % 2 == 0:
                    nc.vector.tensor_copy(result[:], banks[h][m][:])
                else:
                    nc.scalar.copy(result[:], banks[h][m][:])
                nc.sync.dma_start(out[m * P : (m + 1) * P, h * HALF : (h + 1) * HALF], result[:])
